import numpy as np
import ml_dtypes


def mxq(x, axis, fmt="e4m3"):
    dtype, down = {"e4m3": (ml_dtypes.float8_e4m3fn, 7), "e5m2": (ml_dtypes.float8_e5m2, 14)}[fmt]
    v = np.moveaxis(np.asarray(x, np.float32).astype(ml_dtypes.bfloat16).astype(np.float64), axis, -1)
    blocks = v.reshape(v.shape[:-1] + (-1, 32))
    amax = np.abs(blocks).max(-1, keepdims=True)
    byte = np.maximum(np.where(amax > 0, np.frexp(amax)[1] - 1 + 127, 0) - down, 1)
    scale = np.exp2(byte - 127.0)
    codes = (blocks / scale).astype(np.float32).astype(dtype).astype(np.float64)
    return np.moveaxis((codes * scale).reshape(v.shape), -1, axis)


WIDE = False


def mx_kscale(k):
    if not WIDE:
        return np.ones(k)
    levels = np.array([10, -10, 5, -5, 0])
    if k % 512:
        return np.exp2(np.random.permutation(np.resize(levels, k // 32))).repeat(32)
    a = np.empty((k // 512, 16))
    for p in range(k // 512):
        a[p, :8] = np.random.permutation(np.resize(levels, 8))
        for g in range(8):
            far = levels[np.abs(levels - a[p, g]) >= 10]
            a[p, g + 8] = far[np.random.randint(len(far))]
    return np.exp2(a.ravel()).repeat(32)


def f64(x):
    return np.asarray(x).astype(np.float64)


def striped(idx):
    return np.tile(idx.reshape(-1, 16).T, (8, 1)).astype(np.uint16)


def unstriped(offs):
    return offs[:16].T.reshape(-1).astype(np.int64)


E2M1 = np.array([0.0, 0.5, 1.0, 1.5, 2.0, 3.0, 4.0, 6.0, -0.0, -0.5, -1.0, -1.5, -2.0, -3.0, -4.0, -6.0])


def pack_weight(w, fmt):
    k, n = w.shape
    w = f64(np.asarray(w, np.float32).astype(ml_dtypes.bfloat16)).reshape(k // 32, 32, n)
    amax = np.abs(w).max(1)
    if fmt == "e4m3":
        byte = np.frexp(amax)[1] - 1 + 127 - 7
    else:
        mant, ex = np.frexp(amax / 6.0)
        byte = np.where(mant > 0.5, ex, ex - 1) + 127
    byte = np.clip(np.where(amax > 0, byte, 1), 1, 254)
    scaled = (w * np.exp2(127.0 - byte)[:, None, :]).reshape(k, n).astype(np.float32)
    by_word = np.ascontiguousarray(scaled.reshape(k // 512, 128, 4, n).transpose(0, 1, 3, 2))
    if fmt == "e4m3":
        words = by_word.astype(ml_dtypes.float8_e4m3fn).view(np.uint8)
    else:
        c = by_word.astype(ml_dtypes.float4_e2m1fn).view(np.uint8) & 0xF
        words = (c[..., 0::2] | (c[..., 1::2] << 4)).reshape(k // 512, 128, 2 * n)
    return np.ascontiguousarray(words), np.ascontiguousarray(byte.astype(np.uint8).reshape(k // 512, 16, n))


def unpack_weight(words, scales, fmt):
    g, _, n = scales.shape
    words = np.ascontiguousarray(words).reshape(g, 128, n, -1)
    if fmt == "e4m3":
        vals = words.view(ml_dtypes.float8_e4m3fn).astype(np.float64)
    else:
        nib = np.empty((g, 128, n, 4), np.uint8)
        nib[..., 0::2] = words & 0xF
        nib[..., 1::2] = words >> 4
        vals = E2M1[nib]
    vals = vals * np.repeat(np.exp2(scales.astype(np.float64) - 127.0), 8, axis=1)[..., None]
    return vals.transpose(0, 1, 3, 2).reshape(g * 512, n)


def relu2(v):
    return np.maximum(v, 0.0) ** 2


K, T, E, C, H, N = 1024, 640, 2, 256, 1024, 384


def by_expert(wq, xq):
    return np.concatenate([wq[e].T @ xq[:, e * C:(e + 1) * C] for e in range(E)], axis=1)


def setup_inputs():
    n = np.random.standard_normal
    s = mx_kscale(K)[:, None]
    u = mx_kscale(H)
    w1 = [pack_weight(m, "e2m1") for m in n((E, K, H)) / np.sqrt(K) / s[None] * u[None, None, :]]
    w2 = [pack_weight(m, "e2m1") for m in n((E, H, N)) / np.sqrt(H) / u[None, :, None] ** 2]
    return {
        "xT": (n((K, T)) * s).astype(np.float32),
        "xr": n((N, T)).astype(np.float32),
        "w1_words": np.stack([m[0] for m in w1]),
        "w1_scales": np.stack([m[1] for m in w1]),
        "w2_words": np.stack([m[0] for m in w2]),
        "w2_scales": np.stack([m[1] for m in w2]),
        "gate": np.tile(np.random.uniform(0.2, 1.0, E * C), (N, 1)).astype(np.float32),
        "offs": striped(np.random.permutation(T)[:E * C]),
    }


def reference(xT, xr, w1_words, w1_scales, w2_words, w2_scales, gate, offs):
    idx = unstriped(offs)
    w1 = np.stack([unpack_weight(w1_words[e], w1_scales[e], "e2m1") for e in range(E)])
    w2 = np.stack([unpack_weight(w2_words[e], w2_scales[e], "e2m1") for e in range(E)])
    xq = mxq(f64(xT)[:, idx], 0, "e4m3")
    h = relu2(by_expert(w1, xq))
    y = by_expert(w2, mxq(h, 0, "e4m3"))
    out = f64(xr).copy()
    out[:, idx] += f64(gate) * y
    return out

@@ -1,0 +1,217 @@
+from contextlib import ExitStack
+
+import concourse.mybir as mybir
+from concourse.masks import make_identity
+
+K, T, E, C, H, N = 1024, 640, 2, 256, 1024, 384
+S = E * C
+FLOPS = 2 * S * (K * H + H * N)
+
+F32 = mybir.dt.float32
+BF16 = mybir.dt.bfloat16
+I32 = mybir.dt.int32
+U32 = mybir.dt.uint32
+U16 = mybir.dt.uint16
+U8 = mybir.dt.uint8
+E4M3 = mybir.dt.float8_e4m3fn_x4
+E2M1 = mybir.dt.float4_e2m1fn_x4
+ACT = mybir.ActivationFunctionType
+ALU = mybir.AluOpType
+
+P = 128
+KP = K // 512
+HP = H // 512
+ST = S // P
+NT = N // P
+
+CHUNKS = ((0, 384), (384, 640))
+SCALAR_SHARE = {(0, 0): 256, (0, 1): 128, (1, 0): 384, (1, 1): 160}
+QCOLS = (((0, 256), (256, 384)), ((384, 640),))
+VECTOR_RELUS = {(0, 1), (1, 1)}
+
+
+def tile_moe_res_mlp_relu2_kernel(tc, xT, xr, w1_words, w1_scales, w2_words, w2_scales, gate, offs, out):
+    nc = tc.nc
+    with ExitStack() as ctx:
+        keep = ctx.enter_context(tc.tile_pool(name="keep", bufs=1))
+        work = ctx.enter_context(tc.tile_pool(name="work", bufs=3))
+        ps_a = ctx.enter_context(tc.psum_pool(name="ps_a", bufs=3))
+        ps_t = ctx.enter_context(tc.psum_pool(name="ps_t", bufs=3))
+        ps_y = ctx.enter_context(tc.psum_pool(name="ps_y", bufs=2))
+
+        offsets = keep.tile([P, S // 16], U16, name="offsets")
+        nc.sync.dma_start(offsets[:], offs)
+
+        raw = {}
+        for s in range(KP):
+            rows = xT[s * 512 : (s + 1) * 512, :].rearrange("(q j) w -> q j w", j=4)
+            for c, (c0, c1) in enumerate(CHUNKS):
+                t = keep.tile([P, 4, c1 - c0], F32, name=f"raw{s}_{c}")
+                nc.sync.dma_start(out=t[:], in_=rows[:, :, c0:c1])
+                raw[s, c] = t
+
+        ident = keep.tile([P, P], F32, name="ident")
+        make_identity(nc, ident[:])
+        x_scales = [keep.tile([P, T], U8, name=f"x_scales{s}", align_bytes=64) for s in range(KP)]
+        for s in range(KP):
+            nc.gpsimd.memset(x_scales[s][:], 0)
+        w1s = keep.tile([P, E * KP, H], U8, name="w1s", align_bytes=64)
+        w2s = keep.tile([P, E * HP, N], U8, name="w2s", align_bytes=64)
+        nc.vector.memset(w1s[:].rearrange("p g i -> p (g i)").bitcast(I32), 0)
+        nc.vector.memset(w2s[:].rearrange("p g i -> p (g i)").bitcast(I32), 0)
+        warm = keep.tile([P, 1], F32, name="warm")
+        nc.vector.memset(warm[:], 0.0)
+        nc.scalar.activation(warm[:], warm[:], ACT.Square)
+        windows = [keep.tile([P, T], F32, name=f"window{n}") for n in range(NT)]
+        for n in range(NT):
+            nc.vector.memset(windows[n][:], 0.0)
+
+        w1s_rows = w1_scales.bitcast(I32).rearrange("e s q i -> q (e s) i")
+        w2s_rows = w2_scales.bitcast(I32).rearrange("e s q i -> q (e s) i")
+        for q in range(4):
+            nc.gpsimd.dma_start(out=w1s[32 * q : 32 * q + 4, :, :].bitcast(I32), in_=w1s_rows[4 * q : 4 * q + 4, :, :])
+        for q in range(4):
+            nc.gpsimd.dma_start(out=w2s[32 * q : 32 * q + 4, :, :].bitcast(I32), in_=w2s_rows[4 * q : 4 * q + 4, :, :])
+
+        w1w = [keep.tile([P, KP, 2 * H], U8, name=f"w1w{e}", align_bytes=64) for e in range(E)]
+        w1_rows = w1_words.bitcast(I32).rearrange("e s p w -> e p s w")
+        for e in range(E):
+            nc.sync.dma_start(out=w1w[e][:].bitcast(I32), in_=w1_rows[e])
+        w2w = keep.tile([P, E * HP, 2 * N], U8, name="w2w", align_bytes=64)
+        nc.sync.dma_start(out=w2w[:].bitcast(I32), in_=w2_words.bitcast(I32).rearrange("e s p w -> p (e s) w"))
+        gates = keep.tile([P, NT, S], F32, name="gates")
+        nc.sync.dma_start(out=gates[:], in_=gate.rearrange("(n p) s -> p n s", p=P))
+        residual = [keep.tile([P, T], F32, name=f"residual{n}") for n in range(NT)]
+        for n in range(NT):
+            nc.sync.dma_start(out=residual[n][:], in_=xr[n * P : (n + 1) * P, :])
+
+        grouped = [keep.tile([P, T, 4], BF16, name=f"grouped{s}", align_bytes=64) for s in range(KP)]
+        x_words = [keep.tile([P, T], U32, name=f"x_words{s}", align_bytes=64) for s in range(KP)]
+        g_words = {}
+        g_scales = {}
+        for s in range(KP):
+            for e in range(E):
+                g_words[s, e] = keep.tile([P, C], U32, name=f"g_words{s}_{e}", align_bytes=64)
+                g_scales[s, e] = keep.tile([P, C], U8, name=f"g_scales{s}_{e}", align_bytes=64)
+
+        def group_tokens(s):
+            for c, (c0, c1) in enumerate(CHUNKS):
+                src = raw[s, c][:].rearrange("p j w -> p w j")
+                share = SCALAR_SHARE[s, c]
+                nc.scalar.activation(grouped[s][:, c0 : c0 + share, :], src[:, :share, :], ACT.Copy)
+                if c0 + share < c1:
+                    nc.vector.tensor_copy(out=grouped[s][:, c0 + share : c1, :], in_=src[:, share:, :])
+
+        def quantize_tokens(s):
+            for c0, c1 in QCOLS[0] + QCOLS[1]:
+                nc.vector.quantize_mx(
+                    out=x_words[s][:, c0:c1].bitcast(E4M3),
+                    scales=x_scales[s][:, c0:c1],
+                    in_=grouped[s][:, c0:c1, :].rearrange("p w j -> p (w j)"),
+                )
+
+        def gather_tokens(s, e):
+            lists = offsets[:, e * C // 16 : (e + 1) * C // 16]
+            nc.vector.tensor_copy(out=g_words[s, e][:], in_=x_words[s][:].indirect(lists))
+            nc.vector.tensor_copy(out=g_scales[s, e][:], in_=x_scales[s][:].indirect(lists))
+
+        group_tokens(0)
+        quantize_tokens(0)
+        gather_tokens(0, 0)
+        gather_tokens(0, 1)
+        group_tokens(1)
+        quantize_tokens(1)
+        gather_tokens(1, 0)
+        gather_tokens(1, 1)
+
+        def first_product(st):
+            e, c0 = st // 2, (st % 2) * P
+            relus = []
+            for g in range(HP):
+                bank = ps_a.tile([P, 512], F32, name="bank_a")
+                for s in range(KP):
+                    nc.tensor.matmul_mx(
+                        out=bank[:],
+                        lhsT=g_words[s, e][:, c0 : c0 + P].bitcast(E4M3),
+                        lhsT_scale=g_scales[s, e][:, c0 : c0 + P],
+                        rhs=w1w[e][:, s, g * 1024 : (g + 1) * 1024].bitcast(E2M1),
+                        rhs_scale=w1s[:, e * KP + s, g * 512 : (g + 1) * 512],
+                        start=(s == 0),
+                        stop=(s == KP - 1),
+                    )
+                r = work.tile([P, 4, P], F32, name=f"relu{g}")
+                src = bank[:].rearrange("p (m t) -> p t m", t=4)
+                if (st, g) in VECTOR_RELUS:
+                    nc.vector.tensor_scalar_max(r[:], src, 0.0)
+                else:
+                    nc.scalar.activation(r[:], src, ACT.Relu)
+                relus.append(r)
+            return relus
+
+        def turn_and_square(st, relus):
+            h = work.tile([P, HP, P, 4], BF16, name="h", align_bytes=64)
+            for g in range(HP):
+                bank = ps_t.tile([P, 4, P], F32, name="bank_t")
+                for t in range(4):
+                    nc.tensor.transpose(bank[:, t, :], relus[g][:, t, :], ident[:])
+                nc.scalar.activation(h[:, g, :, :], bank[:].rearrange("p t c -> p c t"), ACT.Square)
+            return h
+
+        def quantize_hidden(h):
+            h_words = work.tile([P, HP, P], U32, name="h_words", align_bytes=64)
+            h_scales = work.tile([P, HP, P], U8, name="h_scales", align_bytes=64)
+            nc.vector.quantize_mx(
+                out=h_words[:].rearrange("p g c -> p (g c)").bitcast(E4M3),
+                scales=h_scales[:].rearrange("p g c -> p (g c)"),
+                in_=h[:].rearrange("p g c t -> p (g c t)"),
+            )
+            return h_words, h_scales
+
+        def second_product(st, h_words, h_scales):
+            e = st // 2
+            bank = ps_y.tile([P, NT, P], F32, name="bank_y")
+            for n in range(NT):
+                for g in range(HP):
+                    nc.tensor.matmul_mx(
+                        out=bank[:, n, :],
+                        lhsT=w2w[:, e * HP + g, 256 * n : 256 * (n + 1)].bitcast(E2M1),
+                        lhsT_scale=w2s[:, e * HP + g, P * n : P * (n + 1)],
+                        rhs=h_words[:, g, :].bitcast(E4M3),
+                        rhs_scale=h_scales[:, g, :],
+                        start=(g == 0),
+                        stop=(g == HP - 1),
+                    )
+            y = work.tile([P, NT, P], F32, name="y")
+            nc.scalar.activation(y[:], bank[:], ACT.Copy)
+            return y
+
+        def scatter(st, y, n):
+            nc.vector.tensor_tensor(
+                windows[n][:].indirect(offsets[:, st * 8 : (st + 1) * 8]),
+                y[:, n, :],
+                gates[:, n, st * P : (st + 1) * P],
+                ALU.mult,
+            )
+
+        relus = first_product(0)
+        for st in range(ST):
+            following = first_product(st + 1) if st + 1 < ST else None
+            h = turn_and_square(st, relus)
+            h_words, h_scales = quantize_hidden(h)
+            y = second_product(st, h_words, h_scales)
+            if st + 1 < ST:
+                for n in range(NT):
+                    scatter(st, y, n)
+            relus = following
+
+        def finish(n, c0, c1):
+            nc.vector.tensor_add(out=residual[n][:, c0:c1], in0=windows[n][:, c0:c1], in1=residual[n][:, c0:c1])
+            nc.sync.dma_start(out=out[n * P : (n + 1) * P, c0:c1], in_=residual[n][:, c0:c1])
+
+        scatter(ST - 1, y, 0)
+        scatter(ST - 1, y, 1)
+        finish(0, 0, T)
+        scatter(ST - 1, y, 2)
+        finish(1, 0, T)
+        finish(2, 0, T // 2)
+        finish(2, T // 2, T)

@@ -28,6 +28,8 @@ CHUNKS = ((0, 384), (384, 640))
 SCALAR_SHARE = {(0, 0): 256, (0, 1): 128, (1, 0): 384, (1, 1): 160}
 QCOLS = (((0, 256), (256, 384)), ((384, 640),))
 VECTOR_RELUS = {(0, 1), (1, 1)}
+H_SLOT = ("h0", "h1", "h2", "h3")
+Y_SLOT = ("h1", "h3")
 
 
 def tile_moe_res_mlp_relu2_kernel(tc, xT, xr, w1_words, w1_scales, w2_words, w2_scales, gate, offs, out):
@@ -36,8 +38,8 @@ def tile_moe_res_mlp_relu2_kernel(tc, xT, xr, w1_words, w1_scales, w2_words, w2_
         keep = ctx.enter_context(tc.tile_pool(name="keep", bufs=1))
         work = ctx.enter_context(tc.tile_pool(name="work", bufs=3))
         ps_a = ctx.enter_context(tc.psum_pool(name="ps_a", bufs=3))
-        ps_t = ctx.enter_context(tc.psum_pool(name="ps_t", bufs=3))
-        ps_y = ctx.enter_context(tc.psum_pool(name="ps_y", bufs=2))
+        ps_t = ctx.enter_context(tc.psum_pool(name="ps_t", bufs=2))
+        ps_y = ctx.enter_context(tc.psum_pool(name="ps_y", bufs=3))
 
         offsets = keep.tile([P, S // 16], U16, name="offsets")
         nc.sync.dma_start(offsets[:], offs)
@@ -69,7 +71,7 @@ def tile_moe_res_mlp_relu2_kernel(tc, xT, xr, w1_words, w1_scales, w2_words, w2_
         w1s_rows = w1_scales.bitcast(I32).rearrange("e s q i -> q (e s) i")
         w2s_rows = w2_scales.bitcast(I32).rearrange("e s q i -> q (e s) i")
         for q in range(4):
-            nc.gpsimd.dma_start(out=w1s[32 * q : 32 * q + 4, :, :].bitcast(I32), in_=w1s_rows[4 * q : 4 * q + 4, :, :])
+            nc.sync.dma_start(out=w1s[32 * q : 32 * q + 4, :, :].bitcast(I32), in_=w1s_rows[4 * q : 4 * q + 4, :, :])
         for q in range(4):
             nc.gpsimd.dma_start(out=w2s[32 * q : 32 * q + 4, :, :].bitcast(I32), in_=w2s_rows[4 * q : 4 * q + 4, :, :])
 
@@ -110,28 +112,30 @@ def tile_moe_res_mlp_relu2_kernel(tc, xT, xr, w1_words, w1_scales, w2_words, w2_
                     in_=grouped[s][:, c0:c1, :].rearrange("p w j -> p (w j)"),
                 )
 
-        def gather_tokens(s, e):
-            lists = offsets[:, e * C // 16 : (e + 1) * C // 16]
-            nc.vector.tensor_copy(out=g_words[s, e][:], in_=x_words[s][:].indirect(lists))
-            nc.vector.tensor_copy(out=g_scales[s, e][:], in_=x_scales[s][:].indirect(lists))
+        def gather_tokens(s, j0, j1):
+            e, i0, i1 = j0 // C, j0 % C, (j1 - 1) % C + 1
+            lists = offsets[:, j0 // 16 : j1 // 16]
+            nc.vector.tensor_copy(out=g_words[s, e][:, i0:i1], in_=x_words[s][:].indirect(lists))
+            nc.vector.tensor_copy(out=g_scales[s, e][:, i0:i1], in_=x_scales[s][:].indirect(lists))
 
         group_tokens(0)
         quantize_tokens(0)
-        gather_tokens(0, 0)
-        gather_tokens(0, 1)
+        gather_tokens(0, 0, C)
+        gather_tokens(0, C, S)
         group_tokens(1)
         quantize_tokens(1)
-        gather_tokens(1, 0)
-        gather_tokens(1, 1)
+        gather_tokens(1, 0, P)
+        gather_tokens(1, P, C)
+        gather_tokens(1, C, S)
 
         def first_product(st):
             e, c0 = st // 2, (st % 2) * P
             relus = []
-            for g in range(HP):
-                bank = ps_a.tile([P, 512], F32, name="bank_a")
-                for s in range(KP):
+            banks = [ps_a.tile([P, 512], F32, name="bank_a") for g in range(HP)]
+            for s in range(KP):
+                for g in range(HP):
                     nc.tensor.matmul_mx(
-                        out=bank[:],
+                        out=banks[g][:],
                         lhsT=g_words[s, e][:, c0 : c0 + P].bitcast(E4M3),
                         lhsT_scale=g_scales[s, e][:, c0 : c0 + P],
                         rhs=w1w[e][:, s, g * 1024 : (g + 1) * 1024].bitcast(E2M1),
@@ -139,8 +143,9 @@ def tile_moe_res_mlp_relu2_kernel(tc, xT, xr, w1_words, w1_scales, w2_words, w2_
                         start=(s == 0),
                         stop=(s == KP - 1),
                     )
+            for g in range(HP):
                 r = work.tile([P, 4, P], F32, name=f"relu{g}")
-                src = bank[:].rearrange("p (m t) -> p t m", t=4)
+                src = banks[g][:].rearrange("p (m t) -> p t m", t=4)
                 if (st, g) in VECTOR_RELUS:
                     nc.vector.tensor_scalar_max(r[:], src, 0.0)
                 else:
@@ -149,7 +154,7 @@ def tile_moe_res_mlp_relu2_kernel(tc, xT, xr, w1_words, w1_scales, w2_words, w2_
             return relus
 
         def turn_and_square(st, relus):
-            h = work.tile([P, HP, P, 4], BF16, name="h", align_bytes=64)
+            h = keep.tile([P, HP, P, 4], BF16, name="h", tag=H_SLOT[st], align_bytes=64)
             for g in range(HP):
                 bank = ps_t.tile([P, 4, P], F32, name="bank_t")
                 for t in range(4):
@@ -181,37 +186,48 @@ def tile_moe_res_mlp_relu2_kernel(tc, xT, xr, w1_words, w1_scales, w2_words, w2_
                         start=(g == 0),
                         stop=(g == HP - 1),
                     )
-            y = work.tile([P, NT, P], F32, name="y")
+            return bank
+
+        def empty(st, bank):
+            y = keep.tile([P, NT, P], F32, name="y", tag=Y_SLOT[st], align_bytes=64)
             nc.scalar.activation(y[:], bank[:], ACT.Copy)
             return y
 
-        def scatter(st, y, n):
+        def scatter(j0, j1, y, n):
             nc.vector.tensor_tensor(
-                windows[n][:].indirect(offsets[:, st * 8 : (st + 1) * 8]),
+                windows[n][:].indirect(offsets[:, j0 // 16 : j1 // 16]),
                 y[:, n, :],
-                gates[:, n, st * P : (st + 1) * P],
+                gates[:, n, j0:j1],
                 ALU.mult,
             )
 
-        relus = first_product(0)
-        for st in range(ST):
-            following = first_product(st + 1) if st + 1 < ST else None
-            h = turn_and_square(st, relus)
-            h_words, h_scales = quantize_hidden(h)
-            y = second_product(st, h_words, h_scales)
-            if st + 1 < ST:
-                for n in range(NT):
-                    scatter(st, y, n)
-            relus = following
+        def hidden(st, relus):
+            return second_product(st, *quantize_hidden(turn_and_square(st, relus)))
+
+        def scatter_all(st, y):
+            for n in range(NT):
+                scatter(st * P, (st + 1) * P, y, n)
+
+        relus = [first_product(0), first_product(1)]
+        banks = [hidden(0, relus[0]), hidden(1, relus[1])]
+        relus.append(first_product(2))
+        scatter_all(0, empty(0, banks[0]))
+        banks.append(hidden(2, relus[2]))
+        relus.append(first_product(3))
+        y_last = keep.tile([P, NT, C], F32, name="y_last")
+        nc.scalar.activation(y_last[:, :, 0:P], banks[2][:], ACT.Copy)
+        banks.append(hidden(3, relus[3]))
+        scatter_all(1, empty(1, banks[1]))
+        nc.scalar.activation(y_last[:, :, P:C], banks[3][:], ACT.Copy)
 
         def finish(n, c0, c1):
             nc.vector.tensor_add(out=residual[n][:, c0:c1], in0=windows[n][:, c0:c1], in1=residual[n][:, c0:c1])
             nc.sync.dma_start(out=out[n * P : (n + 1) * P, c0:c1], in_=residual[n][:, c0:c1])
 
-        scatter(ST - 1, y, 0)
-        scatter(ST - 1, y, 1)
+        scatter(C, S, y_last, 0)
+        scatter(C, S, y_last, 1)
         finish(0, 0, T)
-        scatter(ST - 1, y, 2)
+        scatter(C, S, y_last, 2)
         finish(1, 0, T)
         finish(2, 0, T // 2)
         finish(2, T // 2, T)

@@ -24,8 +24,8 @@ HP = H // 512
 ST = S // P
 NT = N // P
 
-CHUNKS = ((0, 384), (384, 640))
-SCALAR_SHARE = {(0, 0): 256, (0, 1): 128, (1, 0): 384, (1, 1): 160}
+CHUNKS = (((0, 640),), ((0, 384), (384, 640)))
+SCALAR_SHARE = {(0, 0): 256, (1, 0): 384, (1, 1): 128}
 QCOLS = (((0, 256), (256, 384)), ((384, 640),))
 VECTOR_RELUS = {(0, 1), (1, 1)}
 H_SLOT = ("h0", "h1", "h2", "h3")
@@ -47,7 +47,7 @@ def tile_moe_res_mlp_relu2_kernel(tc, xT, xr, w1_words, w1_scales, w2_words, w2_
         raw = {}
         for s in range(KP):
             rows = xT[s * 512 : (s + 1) * 512, :].rearrange("(q j) w -> q j w", j=4)
-            for c, (c0, c1) in enumerate(CHUNKS):
+            for c, (c0, c1) in enumerate(CHUNKS[s]):
                 t = keep.tile([P, 4, c1 - c0], F32, name=f"raw{s}_{c}")
                 nc.sync.dma_start(out=t[:], in_=rows[:, :, c0:c1])
                 raw[s, c] = t
@@ -72,13 +72,13 @@ def tile_moe_res_mlp_relu2_kernel(tc, xT, xr, w1_words, w1_scales, w2_words, w2_
         w2s_rows = w2_scales.bitcast(I32).rearrange("e s q i -> q (e s) i")
         for q in range(4):
             nc.sync.dma_start(out=w1s[32 * q : 32 * q + 4, :, :].bitcast(I32), in_=w1s_rows[4 * q : 4 * q + 4, :, :])
-        for q in range(4):
-            nc.gpsimd.dma_start(out=w2s[32 * q : 32 * q + 4, :, :].bitcast(I32), in_=w2s_rows[4 * q : 4 * q + 4, :, :])
 
         w1w = [keep.tile([P, KP, 2 * H], U8, name=f"w1w{e}", align_bytes=64) for e in range(E)]
         w1_rows = w1_words.bitcast(I32).rearrange("e s p w -> e p s w")
         for e in range(E):
             nc.sync.dma_start(out=w1w[e][:].bitcast(I32), in_=w1_rows[e])
+        for q in range(4):
+            nc.sync.dma_start(out=w2s[32 * q : 32 * q + 4, :, :].bitcast(I32), in_=w2s_rows[4 * q : 4 * q + 4, :, :])
         w2w = keep.tile([P, E * HP, 2 * N], U8, name="w2w", align_bytes=64)
         nc.sync.dma_start(out=w2w[:].bitcast(I32), in_=w2_words.bitcast(I32).rearrange("e s p w -> p (e s) w"))
         gates = keep.tile([P, NT, S], F32, name="gates")
@@ -97,7 +97,7 @@ def tile_moe_res_mlp_relu2_kernel(tc, xT, xr, w1_words, w1_scales, w2_words, w2_
                 g_scales[s, e] = keep.tile([P, C], U8, name=f"g_scales{s}_{e}", align_bytes=64)
 
         def group_tokens(s):
-            for c, (c0, c1) in enumerate(CHUNKS):
+            for c, (c0, c1) in enumerate(CHUNKS[s]):
                 src = raw[s, c][:].rearrange("p j w -> p w j")
                 share = SCALAR_SHARE[s, c]
                 nc.scalar.activation(grouped[s][:, c0 : c0 + share, :], src[:, :share, :], ACT.Copy)
@@ -188,18 +188,16 @@ def tile_moe_res_mlp_relu2_kernel(tc, xT, xr, w1_words, w1_scales, w2_words, w2_
                     )
             return bank
 
+        def weigh(st, y, bank):
+            nc.vector.tensor_tensor(y, bank[:], gates[:, :, st * P : (st + 1) * P], ALU.mult)
+
         def empty(st, bank):
             y = keep.tile([P, NT, P], F32, name="y", tag=Y_SLOT[st], align_bytes=64)
-            nc.scalar.activation(y[:], bank[:], ACT.Copy)
+            weigh(st, y[:], bank)
             return y
 
         def scatter(j0, j1, y, n):
-            nc.vector.tensor_tensor(
-                windows[n][:].indirect(offsets[:, j0 // 16 : j1 // 16]),
-                y[:, n, :],
-                gates[:, n, j0:j1],
-                ALU.mult,
-            )
+            nc.vector.tensor_copy(out=windows[n][:].indirect(offsets[:, j0 // 16 : j1 // 16]), in_=y[:, n, :])
 
         def hidden(st, relus):
             return second_product(st, *quantize_hidden(turn_and_square(st, relus)))
@@ -215,10 +213,10 @@ def tile_moe_res_mlp_relu2_kernel(tc, xT, xr, w1_words, w1_scales, w2_words, w2_
         banks.append(hidden(2, relus[2]))
         relus.append(first_product(3))
         y_last = keep.tile([P, NT, C], F32, name="y_last")
-        nc.scalar.activation(y_last[:, :, 0:P], banks[2][:], ACT.Copy)
+        weigh(2, y_last[:, :, 0:P], banks[2])
         banks.append(hidden(3, relus[3]))
         scatter_all(1, empty(1, banks[1]))
-        nc.scalar.activation(y_last[:, :, P:C], banks[3][:], ACT.Copy)
+        weigh(3, y_last[:, :, P:C], banks[3])
 
         def finish(n, c0, c1):
             nc.vector.tensor_add(out=residual[n][:, c0:c1], in0=windows[n][:, c0:c1], in1=residual[n][:, c0:c1])

@@ -27,9 +27,8 @@ NT = N // P
 CHUNKS = (((0, 640),), ((0, 384), (384, 640)))
 SCALAR_SHARE = {(0, 0): 256, (1, 0): 384, (1, 1): 128}
 QCOLS = (((0, 256), (256, 384)), ((384, 640),))
-VECTOR_RELUS = {(0, 1), (1, 1)}
 H_SLOT = ("h0", "h1", "h2", "h3")
-Y_SLOT = ("h1", "h3")
+Y_SLOT = ("h1", "h2", "h3", "y3")
 
 
 def tile_moe_res_mlp_relu2_kernel(tc, xT, xr, w1_words, w1_scales, w2_words, w2_scales, gate, offs, out):
@@ -42,7 +41,6 @@ def tile_moe_res_mlp_relu2_kernel(tc, xT, xr, w1_words, w1_scales, w2_words, w2_
         ps_y = ctx.enter_context(tc.psum_pool(name="ps_y", bufs=3))
 
         offsets = keep.tile([P, S // 16], U16, name="offsets")
-        nc.sync.dma_start(offsets[:], offs)
 
         raw = {}
         for s in range(KP):
@@ -51,6 +49,8 @@ def tile_moe_res_mlp_relu2_kernel(tc, xT, xr, w1_words, w1_scales, w2_words, w2_
                 t = keep.tile([P, 4, c1 - c0], F32, name=f"raw{s}_{c}")
                 nc.sync.dma_start(out=t[:], in_=rows[:, :, c0:c1])
                 raw[s, c] = t
+            if s == 0:
+                nc.sync.dma_start(offsets[:], offs)
 
         ident = keep.tile([P, P], F32, name="ident")
         make_identity(nc, ident[:])
@@ -146,10 +146,7 @@ def tile_moe_res_mlp_relu2_kernel(tc, xT, xr, w1_words, w1_scales, w2_words, w2_
             for g in range(HP):
                 r = work.tile([P, 4, P], F32, name=f"relu{g}")
                 src = banks[g][:].rearrange("p (m t) -> p t m", t=4)
-                if (st, g) in VECTOR_RELUS:
-                    nc.vector.tensor_scalar_max(r[:], src, 0.0)
-                else:
-                    nc.scalar.activation(r[:], src, ACT.Relu)
+                nc.scalar.activation(r[:], src, ACT.Relu)
                 relus.append(r)
             return relus
 
@@ -188,16 +185,17 @@ def tile_moe_res_mlp_relu2_kernel(tc, xT, xr, w1_words, w1_scales, w2_words, w2_
                     )
             return bank
 
-        def weigh(st, y, bank):
-            nc.vector.tensor_tensor(y, bank[:], gates[:, :, st * P : (st + 1) * P], ALU.mult)
-
         def empty(st, bank):
-            y = keep.tile([P, NT, P], F32, name="y", tag=Y_SLOT[st], align_bytes=64)
-            weigh(st, y[:], bank)
-            return y
+            first = keep.tile([P, 1, P], F32, name=f"y_first{st}")
+            rest = keep.tile([P, NT - 1, P], F32, name="y_rest", tag=Y_SLOT[st], align_bytes=64)
+            nc.scalar.activation(first[:], bank[:, 0:1, :], ACT.Copy)
+            nc.scalar.activation(rest[:], bank[:, 1:NT, :], ACT.Copy)
+            return [first[:, 0, :], rest[:, 0, :], rest[:, 1, :]]
 
         def scatter(j0, j1, y, n):
-            nc.vector.tensor_copy(out=windows[n][:].indirect(offsets[:, j0 // 16 : j1 // 16]), in_=y[:, n, :])
+            nc.vector.tensor_tensor(
+                windows[n][:].indirect(offsets[:, j0 // 16 : j1 // 16]), y[n], gates[:, n, j0:j1], ALU.mult
+            )
 
         def hidden(st, relus):
             return second_product(st, *quantize_hidden(turn_and_square(st, relus)))
@@ -212,20 +210,19 @@ def tile_moe_res_mlp_relu2_kernel(tc, xT, xr, w1_words, w1_scales, w2_words, w2_
         scatter_all(0, empty(0, banks[0]))
         banks.append(hidden(2, relus[2]))
         relus.append(first_product(3))
-        y_last = keep.tile([P, NT, C], F32, name="y_last")
-        weigh(2, y_last[:, :, 0:P], banks[2])
-        banks.append(hidden(3, relus[3]))
         scatter_all(1, empty(1, banks[1]))
-        weigh(3, y_last[:, :, P:C], banks[3])
+        banks.append(hidden(3, relus[3]))
+        scatter_all(2, empty(2, banks[2]))
+        y = empty(3, banks[3])
 
         def finish(n, c0, c1):
             nc.vector.tensor_add(out=residual[n][:, c0:c1], in0=windows[n][:, c0:c1], in1=residual[n][:, c0:c1])
             nc.sync.dma_start(out=out[n * P : (n + 1) * P, c0:c1], in_=residual[n][:, c0:c1])
 
-        scatter(C, S, y_last, 0)
-        scatter(C, S, y_last, 1)
+        scatter(S - P, S, y, 0)
+        scatter(S - P, S, y, 1)
         finish(0, 0, T)
-        scatter(C, S, y_last, 2)
+        scatter(S - P, S, y, 2)
         finish(1, 0, T)
         finish(2, 0, T // 2)
         finish(2, T // 2, T)

from contextlib import ExitStack

import concourse.mybir as mybir
from concourse.masks import make_identity

K, T, E, C, H, N = 1024, 640, 2, 256, 1024, 384
S = E * C
FLOPS = 2 * S * (K * H + H * N)

F32 = mybir.dt.float32
BF16 = mybir.dt.bfloat16
I32 = mybir.dt.int32
U32 = mybir.dt.uint32
U16 = mybir.dt.uint16
U8 = mybir.dt.uint8
E4M3 = mybir.dt.float8_e4m3fn_x4
E2M1 = mybir.dt.float4_e2m1fn_x4
ACT = mybir.ActivationFunctionType
ALU = mybir.AluOpType

P = 128
KP = K // 512
HP = H // 512
ST = S // P
NT = N // P

CHUNKS = (((0, 640),), ((0, 384), (384, 640)))
SCALAR_SHARE = {(0, 0): 256, (1, 0): 384, (1, 1): 128}
QCOLS = (((0, 256), (256, 384)), ((384, 640),))
H_SLOT = ("h0", "h1", "h2", "h3")
Y_SLOT = ("h1", "h2", "h3", "y3")


def tile_moe_res_mlp_relu2_kernel(tc, xT, xr, w1_words, w1_scales, w2_words, w2_scales, gate, offs, out):
    nc = tc.nc
    with ExitStack() as ctx:
        keep = ctx.enter_context(tc.tile_pool(name="keep", bufs=1))
        work = ctx.enter_context(tc.tile_pool(name="work", bufs=3))
        ps_a = ctx.enter_context(tc.psum_pool(name="ps_a", bufs=3))
        ps_t = ctx.enter_context(tc.psum_pool(name="ps_t", bufs=2))
        ps_y = ctx.enter_context(tc.psum_pool(name="ps_y", bufs=3))

        offsets = keep.tile([P, S // 16], U16, name="offsets")

        raw = {}
        for s in range(KP):
            rows = xT[s * 512 : (s + 1) * 512, :].rearrange("(q j) w -> q j w", j=4)
            for c, (c0, c1) in enumerate(CHUNKS[s]):
                t = keep.tile([P, 4, c1 - c0], F32, name=f"raw{s}_{c}")
                nc.sync.dma_start(out=t[:], in_=rows[:, :, c0:c1])
                raw[s, c] = t
            if s == 0:
                nc.sync.dma_start(offsets[:], offs)

        ident = keep.tile([P, P], F32, name="ident")
        make_identity(nc, ident[:])
        x_scales = [keep.tile([P, T], U8, name=f"x_scales{s}", align_bytes=64) for s in range(KP)]
        for s in range(KP):
            nc.gpsimd.memset(x_scales[s][:], 0)
        w1s = keep.tile([P, E * KP, H], U8, name="w1s", align_bytes=64)
        w2s = keep.tile([P, E * HP, N], U8, name="w2s", align_bytes=64)
        nc.vector.memset(w1s[:].rearrange("p g i -> p (g i)").bitcast(I32), 0)
        nc.vector.memset(w2s[:].rearrange("p g i -> p (g i)").bitcast(I32), 0)
        warm = keep.tile([P, 1], F32, name="warm")
        nc.vector.memset(warm[:], 0.0)
        nc.scalar.activation(warm[:], warm[:], ACT.Square)
        windows = [keep.tile([P, T], F32, name=f"window{n}") for n in range(NT)]
        for n in range(NT):
            nc.vector.memset(windows[n][:], 0.0)

        w1s_rows = w1_scales.bitcast(I32).rearrange("e s q i -> q (e s) i")
        w2s_rows = w2_scales.bitcast(I32).rearrange("e s q i -> q (e s) i")
        for q in range(4):
            nc.sync.dma_start(out=w1s[32 * q : 32 * q + 4, :, :].bitcast(I32), in_=w1s_rows[4 * q : 4 * q + 4, :, :])

        w1w = [keep.tile([P, KP, 2 * H], U8, name=f"w1w{e}", align_bytes=64) for e in range(E)]
        w1_rows = w1_words.bitcast(I32).rearrange("e s p w -> e p s w")
        for e in range(E):
            nc.sync.dma_start(out=w1w[e][:].bitcast(I32), in_=w1_rows[e])
        for q in range(4):
            nc.sync.dma_start(out=w2s[32 * q : 32 * q + 4, :, :].bitcast(I32), in_=w2s_rows[4 * q : 4 * q + 4, :, :])
        w2w = keep.tile([P, E * HP, 2 * N], U8, name="w2w", align_bytes=64)
        nc.sync.dma_start(out=w2w[:].bitcast(I32), in_=w2_words.bitcast(I32).rearrange("e s p w -> p (e s) w"))
        gates = keep.tile([P, NT, S], F32, name="gates")
        nc.sync.dma_start(out=gates[:], in_=gate.rearrange("(n p) s -> p n s", p=P))
        residual = [keep.tile([P, T], F32, name=f"residual{n}") for n in range(NT)]
        for n in range(NT):
            nc.sync.dma_start(out=residual[n][:], in_=xr[n * P : (n + 1) * P, :])

        grouped = [keep.tile([P, T, 4], BF16, name=f"grouped{s}", align_bytes=64) for s in range(KP)]
        x_words = [keep.tile([P, T], U32, name=f"x_words{s}", align_bytes=64) for s in range(KP)]
        g_words = {}
        g_scales = {}
        for s in range(KP):
            for e in range(E):
                g_words[s, e] = keep.tile([P, C], U32, name=f"g_words{s}_{e}", align_bytes=64)
                g_scales[s, e] = keep.tile([P, C], U8, name=f"g_scales{s}_{e}", align_bytes=64)

        def group_tokens(s):
            for c, (c0, c1) in enumerate(CHUNKS[s]):
                src = raw[s, c][:].rearrange("p j w -> p w j")
                share = SCALAR_SHARE[s, c]
                nc.scalar.activation(grouped[s][:, c0 : c0 + share, :], src[:, :share, :], ACT.Copy)
                if c0 + share < c1:
                    nc.vector.tensor_copy(out=grouped[s][:, c0 + share : c1, :], in_=src[:, share:, :])

        def quantize_tokens(s):
            for c0, c1 in QCOLS[0] + QCOLS[1]:
                nc.vector.quantize_mx(
                    out=x_words[s][:, c0:c1].bitcast(E4M3),
                    scales=x_scales[s][:, c0:c1],
                    in_=grouped[s][:, c0:c1, :].rearrange("p w j -> p (w j)"),
                )

        def gather_tokens(s, j0, j1):
            e, i0, i1 = j0 // C, j0 % C, (j1 - 1) % C + 1
            lists = offsets[:, j0 // 16 : j1 // 16]
            nc.vector.tensor_copy(out=g_words[s, e][:, i0:i1], in_=x_words[s][:].indirect(lists))
            nc.vector.tensor_copy(out=g_scales[s, e][:, i0:i1], in_=x_scales[s][:].indirect(lists))

        group_tokens(0)
        quantize_tokens(0)
        gather_tokens(0, 0, C)
        gather_tokens(0, C, S)
        group_tokens(1)
        quantize_tokens(1)
        gather_tokens(1, 0, P)
        gather_tokens(1, P, C)
        gather_tokens(1, C, S)

        def first_product(st):
            e, c0 = st // 2, (st % 2) * P
            relus = []
            banks = [ps_a.tile([P, 512], F32, name="bank_a") for g in range(HP)]
            for s in range(KP):
                for g in range(HP):
                    nc.tensor.matmul_mx(
                        out=banks[g][:],
                        lhsT=g_words[s, e][:, c0 : c0 + P].bitcast(E4M3),
                        lhsT_scale=g_scales[s, e][:, c0 : c0 + P],
                        rhs=w1w[e][:, s, g * 1024 : (g + 1) * 1024].bitcast(E2M1),
                        rhs_scale=w1s[:, e * KP + s, g * 512 : (g + 1) * 512],
                        start=(s == 0),
                        stop=(s == KP - 1),
                    )
            for g in range(HP):
                r = work.tile([P, 4, P], F32, name=f"relu{g}")
                src = banks[g][:].rearrange("p (m t) -> p t m", t=4)
                nc.scalar.activation(r[:], src, ACT.Relu)
                relus.append(r)
            return relus

        def turn_and_square(st, relus):
            h = keep.tile([P, HP, P, 4], BF16, name="h", tag=H_SLOT[st], align_bytes=64)
            for g in range(HP):
                bank = ps_t.tile([P, 4, P], F32, name="bank_t")
                for t in range(4):
                    nc.tensor.transpose(bank[:, t, :], relus[g][:, t, :], ident[:])
                nc.scalar.activation(h[:, g, :, :], bank[:].rearrange("p t c -> p c t"), ACT.Square)
            return h

        def quantize_hidden(h):
            h_words = work.tile([P, HP, P], U32, name="h_words", align_bytes=64)
            h_scales = work.tile([P, HP, P], U8, name="h_scales", align_bytes=64)
            nc.vector.quantize_mx(
                out=h_words[:].rearrange("p g c -> p (g c)").bitcast(E4M3),
                scales=h_scales[:].rearrange("p g c -> p (g c)"),
                in_=h[:].rearrange("p g c t -> p (g c t)"),
            )
            return h_words, h_scales

        def second_product(st, h_words, h_scales):
            e = st // 2
            bank = ps_y.tile([P, NT, P], F32, name="bank_y")
            for n in range(NT):
                for g in range(HP):
                    nc.tensor.matmul_mx(
                        out=bank[:, n, :],
                        lhsT=w2w[:, e * HP + g, 256 * n : 256 * (n + 1)].bitcast(E2M1),
                        lhsT_scale=w2s[:, e * HP + g, P * n : P * (n + 1)],
                        rhs=h_words[:, g, :].bitcast(E4M3),
                        rhs_scale=h_scales[:, g, :],
                        start=(g == 0),
                        stop=(g == HP - 1),
                    )
            return bank

        def empty(st, bank):
            first = keep.tile([P, 1, P], F32, name=f"y_first{st}")
            rest = keep.tile([P, NT - 1, P], F32, name="y_rest", tag=Y_SLOT[st], align_bytes=64)
            nc.scalar.activation(first[:], bank[:, 0:1, :], ACT.Copy)
            nc.scalar.activation(rest[:], bank[:, 1:NT, :], ACT.Copy)
            return [first[:, 0, :], rest[:, 0, :], rest[:, 1, :]]

        def scatter(j0, j1, y, n):
            nc.vector.tensor_tensor(
                windows[n][:].indirect(offsets[:, j0 // 16 : j1 // 16]), y[n], gates[:, n, j0:j1], ALU.mult
            )

        def hidden(st, relus):
            return second_product(st, *quantize_hidden(turn_and_square(st, relus)))

        def scatter_all(st, y):
            for n in range(NT):
                scatter(st * P, (st + 1) * P, y, n)

        relus = [first_product(0), first_product(1)]
        banks = [hidden(0, relus[0]), hidden(1, relus[1])]
        relus.append(first_product(2))
        scatter_all(0, empty(0, banks[0]))
        banks.append(hidden(2, relus[2]))
        relus.append(first_product(3))
        scatter_all(1, empty(1, banks[1]))
        banks.append(hidden(3, relus[3]))
        scatter_all(2, empty(2, banks[2]))
        y = empty(3, banks[3])

        def finish(n, c0, c1):
            nc.vector.tensor_add(out=residual[n][:, c0:c1], in0=windows[n][:, c0:c1], in1=residual[n][:, c0:c1])
            nc.sync.dma_start(out=out[n * P : (n + 1) * P, c0:c1], in_=residual[n][:, c0:c1])

        scatter(S - P, S, y, 0)
        scatter(S - P, S, y, 1)
        finish(0, 0, T)
        scatter(S - P, S, y, 2)
        finish(1, 0, T)
        finish(2, 0, T // 2)
        finish(2, T // 2, T)
